import numpy as np
import ml_dtypes


def mxq(x, axis, fmt="e4m3"):
    dtype, down = {"e4m3": (ml_dtypes.float8_e4m3fn, 7), "e5m2": (ml_dtypes.float8_e5m2, 14)}[fmt]
    v = np.moveaxis(np.asarray(x, np.float32).astype(ml_dtypes.bfloat16).astype(np.float64), axis, -1)
    blocks = v.reshape(v.shape[:-1] + (-1, 32))
    amax = np.abs(blocks).max(-1, keepdims=True)
    byte = np.maximum(np.where(amax > 0, np.frexp(amax)[1] - 1 + 127, 0) - down, 1)
    scale = np.exp2(byte - 127.0)
    codes = (blocks / scale).astype(np.float32).astype(dtype).astype(np.float64)
    return np.moveaxis((codes * scale).reshape(v.shape), -1, axis)


WIDE = False


def mx_kscale(k):
    if not WIDE:
        return np.ones(k)
    levels = np.array([10, -10, 5, -5, 0])
    if k % 512:
        return np.exp2(np.random.permutation(np.resize(levels, k // 32))).repeat(32)
    a = np.empty((k // 512, 16))
    for p in range(k // 512):
        a[p, :8] = np.random.permutation(np.resize(levels, 8))
        for g in range(8):
            far = levels[np.abs(levels - a[p, g]) >= 10]
            a[p, g + 8] = far[np.random.randint(len(far))]
    return np.exp2(a.ravel()).repeat(32)


def f64(x):
    return np.asarray(x).astype(np.float64)


def striped(idx):
    return np.tile(idx.reshape(-1, 16).T, (8, 1)).astype(np.uint16)


def unstriped(offs):
    return offs[:16].T.reshape(-1).astype(np.int64)


E2M1 = np.array([0.0, 0.5, 1.0, 1.5, 2.0, 3.0, 4.0, 6.0, -0.0, -0.5, -1.0, -1.5, -2.0, -3.0, -4.0, -6.0])


def pack_weight(w, fmt):
    k, n = w.shape
    w = f64(np.asarray(w, np.float32).astype(ml_dtypes.bfloat16)).reshape(k // 32, 32, n)
    amax = np.abs(w).max(1)
    if fmt == "e4m3":
        byte = np.frexp(amax)[1] - 1 + 127 - 7
    else:
        mant, ex = np.frexp(amax / 6.0)
        byte = np.where(mant > 0.5, ex, ex - 1) + 127
    byte = np.clip(np.where(amax > 0, byte, 1), 1, 254)
    scaled = (w * np.exp2(127.0 - byte)[:, None, :]).reshape(k, n).astype(np.float32)
    by_word = np.ascontiguousarray(scaled.reshape(k // 512, 128, 4, n).transpose(0, 1, 3, 2))
    if fmt == "e4m3":
        words = by_word.astype(ml_dtypes.float8_e4m3fn).view(np.uint8)
    else:
        c = by_word.astype(ml_dtypes.float4_e2m1fn).view(np.uint8) & 0xF
        words = (c[..., 0::2] | (c[..., 1::2] << 4)).reshape(k // 512, 128, 2 * n)
    return np.ascontiguousarray(words), np.ascontiguousarray(byte.astype(np.uint8).reshape(k // 512, 16, n))


def unpack_weight(words, scales, fmt):
    g, _, n = scales.shape
    words = np.ascontiguousarray(words).reshape(g, 128, n, -1)
    if fmt == "e4m3":
        vals = words.view(ml_dtypes.float8_e4m3fn).astype(np.float64)
    else:
        nib = np.empty((g, 128, n, 4), np.uint8)
        nib[..., 0::2] = words & 0xF
        nib[..., 1::2] = words >> 4
        vals = E2M1[nib]
    vals = vals * np.repeat(np.exp2(scales.astype(np.float64) - 127.0), 8, axis=1)[..., None]
    return vals.transpose(0, 1, 3, 2).reshape(g * 512, n)


def gelu(v):
    return 0.5 * v * (1.0 + np.tanh(np.sqrt(2.0 / np.pi) * (v + 0.044715 * v**3)))


def striped8(idx):
    return np.concatenate([v.reshape(-1, 16).T for v in idx]).astype(np.uint16)


def unstriped8(offs):
    return np.stack([offs[16 * g:16 * g + 16].T.reshape(-1) for g in range(8)]).astype(np.int64)


def put_heads(h, wgs, idx8, t2):
    r = np.arange(h.shape[0])
    page = np.zeros((h.shape[0], t2))
    page[r[:, None], idx8[r % 512 // 64]] = wgs[r // 4 % 128] * h
    return page


K, T, S, T2, P, H, N = 1024, 4096, 1024, 2048, 1024, 512, 768

def setup_inputs():
    n = np.random.standard_normal
    s = mx_kscale(K)[:, None]
    u = mx_kscale(H)[:, None]
    level = np.cos(np.random.uniform(0.0, np.pi, T))
    tab_words, tab_scales = pack_weight((n((K, T)) + level[None, :]) * s, "e4m3")
    w1 = (0.11 * n((K, H)) / np.sqrt(K) + 0.95 * np.sign(n(H))[None, :] / K) / s
    w2_words, w2_scales = pack_weight(n((H, N)) / np.sqrt(H) / u, "e2m1")
    w3_words, w3_scales = pack_weight(0.41 * n((K, N)) / np.sqrt(K) / s, "e4m3")
    return {
        "tab_words": tab_words, "tab_scales": tab_scales,
        "offs": striped(np.random.permutation(T)[:S]),
        "offs2": striped8(np.stack([np.random.permutation(T2)[:S] for _ in range(8)])),
        "offs3": striped(np.random.permutation(T2)[:P]),
        "w1": w1.astype(np.float32),
        "wgs": np.repeat(np.random.uniform(0.5, 2.0, (8, S)), 16, axis=0).astype(np.float32),
        "mat": (n((H, P)) * u).astype(np.float32),
        "gain": (np.exp(0.3 * n(H)) * u[:, 0]).astype(np.float32),
        "w2_words": w2_words, "w2_scales": w2_scales,
        "w3_words": w3_words, "w3_scales": w3_scales,
    }

def reference(tab_words, tab_scales, offs, offs2, offs3, w1, wgs, mat, gain, w2_words, w2_scales, w3_words, w3_scales):
    v = unpack_weight(tab_words, tab_scales, "e4m3")[:, unstriped(offs)]
    y = mxq(f64(w1), 0, "e4m3").T @ v
    h = 0.5 * y * (1.0 + np.tanh(0.7978845608028654 * (y + 0.044715 * y ** 3)))
    page = put_heads(h, f64(wgs), unstriped8(offs2), T2)
    x = page[:, unstriped(offs3)]
    z = np.cos(x) * f64(mat) + f64(gain)[:, None] * x
    e = unpack_weight(w2_words, w2_scales, "e2m1").T @ mxq(z, 0, "e4m3")
    b = unpack_weight(w3_words, w3_scales, "e4m3").T @ v
    return e * np.cos(b)

@@ -1,0 +1,226 @@
+import math
+from contextlib import ExitStack
+
+import concourse.mybir as mybir
+
+K, T, S, T2, H, N = 1024, 4096, 1024, 2048, 512, 768
+FLOPS = 2 * K * H * S + 2 * K * N * S + 2 * H * N * S
+
+F32 = mybir.dt.float32
+BF16 = mybir.dt.bfloat16
+I32 = mybir.dt.int32
+U32 = mybir.dt.uint32
+U16 = mybir.dt.uint16
+U8 = mybir.dt.uint8
+E4M3X4 = mybir.dt.float8_e4m3fn_x4
+E2M1X4 = mybir.dt.float4_e2m1fn_x4
+ALU = mybir.AluOpType
+ACT = mybir.ActivationFunctionType
+
+P = 128
+PACK = 4
+PASSES = K // (P * PACK)
+BANK = 512
+N_TILES = N // P
+CHUNK = 256
+LIST_ROWS = 16
+
+
+def tile_list_seat_coverage_tuner_kernel(
+    tc, tab_words, tab_scales, offs, offs2, offs3, w1, wgs, mat, gain, w2_words, w2_scales, w3_words, w3_scales, out
+):
+    nc = tc.nc
+    with ExitStack() as ctx:
+        keep = ctx.enter_context(tc.tile_pool(name="keep", bufs=1))
+        psum = ctx.enter_context(tc.psum_pool(name="psum", bufs=8))
+
+        def held(name, shape, dtype):
+            return keep.tile(shape, dtype, name=name, align_bytes=64)
+
+        def entries(lst, start, count):
+            return lst[:, start // LIST_ROWS : (start + count) // LIST_ROWS]
+
+        def load_scale_rows(plane, scales, passes):
+            for q in range(4):
+                nc.sync.dma_start(
+                    out=plane[32 * q : 32 * q + 4 * passes, :].bitcast(I32),
+                    in_=scales[:, 4 * q : 4 * q + 4, :].bitcast(I32),
+                )
+
+        def load_words(tile, words):
+            nc.sync.dma_start(out=tile[:].bitcast(I32), in_=words.rearrange("p t i -> p (t i)").bitcast(I32))
+
+        idx = held("idx", [P, S // LIST_ROWS], U16)
+        idx2 = held("idx2", [P, S // LIST_ROWS], U16)
+        idx3 = held("idx3", [P, S // LIST_ROWS], U16)
+        tab_code = [held("tab_code%d" % a, [P, T], U32) for a in range(PASSES)]
+        tab_plane = held("tab_plane", [P, T], U8)
+        v_code = [held("v_code%d" % a, [P, S], U32) for a in range(PASSES)]
+        v_plane = held("v_plane", [P, S], U8)
+        w1_first = held("w1_first", [P, PACK, H], F32)
+        w1_second = [held("w1_second%d" % u, [P, PACK, H // 2], F32) for u in range(2)]
+        w1_bf = [held("w1_bf%d" % a, [P, PACK, P, PACK], BF16) for a in range(PASSES)]
+        w1_code = [held("w1_code%d" % a, [P, H], U32) for a in range(PASSES)]
+        w1_plane = [held("w1_plane%d" % a, [P, H], U8) for a in range(PASSES)]
+        w3_code = [held("w3_code%d" % a, [P, N], U32) for a in range(PASSES)]
+        w3_plane = held("w3_plane", [P, N], U8)
+        w2_code = held("w2_code", [P, 2 * N], U8)
+        w2_plane = held("w2_plane", [P, N], U8)
+        wgs_sb = held("wgs_sb", [P, S], F32)
+        mat_sb = held("mat_sb", [P, PACK, S], F32)
+        gain_sb = held("gain_sb", [P, PACK], F32)
+        h = [held("h%d" % i, [P, S], F32) for i in range(PACK)]
+        page = [held("page%d" % i, [P, T2], F32) for i in range(PACK)]
+        x = held("x", [P, PACK, S], F32)
+        z = held("z", [P, PACK, S], F32)
+        mag = [held("mag%d" % u, [P, S], F32) for u in range(2)]
+        res = held("res", [P, N_TILES, S], F32)
+
+        for plane in (tab_plane, w3_plane, w2_plane):
+            nc.vector.memset(plane[:].bitcast(I32), 0)
+        for i in range(PACK):
+            (nc.vector if i < 2 else nc.gpsimd).memset(page[i][:], 0.0)
+
+        w1_rows = w1.rearrange("(a p j) c -> a p j c", a=PASSES, j=PACK)
+        nc.sync.dma_start(out=idx[:], in_=offs)
+        load_words(tab_code[0], tab_words[0])
+        load_scale_rows(tab_plane, tab_scales, PASSES)
+        nc.sync.dma_start(out=w1_first[:], in_=w1_rows[0])
+        load_words(tab_code[1], tab_words[1])
+        for u in range(2):
+            nc.sync.dma_start(out=w1_second[u][:], in_=w1_rows[1][:, :, u * (H // 2) : (u + 1) * (H // 2)])
+        nc.sync.dma_start(out=wgs_sb[:], in_=wgs)
+        nc.sync.dma_start(out=idx2[:], in_=offs2)
+        for a in range(PASSES):
+            load_words(w3_code[a], w3_words[a])
+        load_scale_rows(w3_plane, w3_scales, PASSES)
+        nc.sync.dma_start(out=idx3[:], in_=offs3)
+        nc.sync.dma_start(out=mat_sb[:], in_=mat.rearrange("(p i) j -> p i j", i=PACK))
+        nc.sync.dma_start(out=gain_sb[:], in_=gain.rearrange("(p i) -> p i", i=PACK))
+        nc.sync.dma_start(out=w2_code[:].bitcast(I32), in_=w2_words[0].bitcast(I32))
+        load_scale_rows(w2_plane, w2_scales, 1)
+
+        nc.vector.tensor_copy(v_code[0][:], tab_code[0][:].indirect(idx[:]))
+        nc.vector.tensor_copy(v_plane[:], tab_plane[:].indirect(idx[:]))
+
+        def deal_w1(copy, a, raw, m0, count):
+            copy(
+                out=w1_bf[a][:, :, m0 : m0 + count, :].rearrange("p i m j -> p m j i"),
+                in_=raw[:].rearrange("p j (m i) -> p m j i", i=PACK),
+            )
+
+        def quantise_w1(a, i0, i1):
+            cols = slice(i0 * P, i1 * P)
+            nc.vector.quantize_mx(
+                out=w1_code[a][:, cols].bitcast(E4M3X4),
+                scales=w1_plane[a][:, cols],
+                in_=w1_bf[a][:, i0:i1, :, :].rearrange("p i m j -> p (i m j)"),
+            )
+
+        deal_w1(nc.scalar.copy, 0, w1_first, 0, P)
+        quantise_w1(0, 0, PACK)
+        nc.vector.tensor_copy(v_code[1][:], tab_code[1][:].indirect(idx[:]))
+        deal_w1(nc.scalar.copy, 1, w1_second[0], 0, P // 2)
+        deal_w1(nc.vector.tensor_copy, 1, w1_second[1], P // 2, P // 2)
+        quantise_w1(1, 0, 1)
+        quantise_w1(1, 1, PACK)
+
+        def times_table(codes, planes, tile, cols):
+            bank = psum.tile([P, BANK], F32, name="bank")
+            m_cols = slice(tile * P, (tile + 1) * P)
+            for a in range(PASSES):
+                nc.tensor.matmul_mx(
+                    out=bank[:],
+                    lhsT=codes[a][:, m_cols].bitcast(E4M3X4),
+                    lhsT_scale=planes[a][:, m_cols],
+                    rhs=v_code[a][:, cols].bitcast(E4M3X4),
+                    rhs_scale=v_plane[4 * a :, cols],
+                    start=(a == 0),
+                    stop=(a == PASSES - 1),
+                )
+            return bank
+
+        halves = [slice(u * BANK, (u + 1) * BANK) for u in range(S // BANK)]
+        for i, u in ((0, 0), (1, 0), (0, 1), (1, 1), (2, 0), (2, 1), (3, 0), (3, 1)):
+            bank = times_table(w1_code, w1_plane, i, halves[u])
+            nc.scalar.activation(out=h[i][:, halves[u]], in_=bank[:], func=ACT.Gelu_apprx_tanh)
+
+        def cosine_of_magnitude(dst, magnitude):
+            nc.scalar.activation(out=dst, in_=magnitude, func=ACT.Sin, scale=-1.0, bias=math.pi / 2)
+
+        w3_planes = [w3_plane[4 * a :, :] for a in range(PASSES)]
+        for n in range(N_TILES):
+            for cols in halves:
+                bank = times_table(w3_code, w3_planes, n, cols)
+                nc.scalar.activation(out=mag[n % 2][:, cols], in_=bank[:], func=ACT.Abs)
+            cosine_of_magnitude(res[:, n, :], mag[n % 2][:])
+
+        def put(i, start, count):
+            cols = slice(start, start + count)
+            nc.vector.tensor_tensor(
+                page[i][:].indirect(entries(idx2, start, count)), h[i][:, cols], wgs_sb[:, cols], ALU.mult
+            )
+
+        def fetch(i, start, count):
+            nc.vector.tensor_copy(x[:, i, start : start + count], page[i][:].indirect(entries(idx3, start, count)))
+
+        for u in range(2):
+            put(0, u * BANK, BANK)
+            put(1, u * BANK, BANK)
+        put(2, 0, S)
+        fetch(0, 0, S)
+        fetch(1, 0, S)
+        fetch(2, 0, S)
+        put(3, 0, S)
+        for u in range(2):
+            fetch(3, u * BANK, BANK)
+
+        def combine(i0, i1, cols):
+            nc.vector.tensor_tensor(z[:, i0:i1, cols], z[:, i0:i1, cols], mat_sb[:, i0:i1, cols], ALU.mult)
+            for i in range(i0, i1):
+                nc.vector.scalar_tensor_tensor(
+                    z[:, i, cols], x[:, i, cols], gain_sb[:, i : i + 1], z[:, i, cols], ALU.mult, ALU.add
+                )
+
+        whole = slice(0, S)
+
+        def cosine(i, cols):
+            nc.scalar.activation(out=mag[i % 2][:, cols], in_=x[:, i, cols], func=ACT.Abs)
+            cosine_of_magnitude(z[:, i, cols], mag[i % 2][:, cols])
+
+        for i in range(3):
+            cosine(i, whole)
+        chunks = [slice(c, c + CHUNK) for c in range(0, S, CHUNK)]
+        for cols in chunks:
+            cosine(3, cols)
+        combine(0, 2, whole)
+
+        out_tiles = out.rearrange("(n p) j -> p n j", p=P)
+        for c, cols in enumerate(chunks):
+            combine(2, 4, cols)
+            z_bf = held("z_bf%d" % c, [P, CHUNK, PACK], BF16)
+            z_code = held("z_code%d" % c, [P, CHUNK], U32)
+            z_plane = held("z_plane%d" % c, [P, CHUNK], U8)
+            nc.scalar.copy(
+                out=z_bf[:].rearrange("p (c f) i -> p c i f", f=4),
+                in_=z[:, :, cols].rearrange("p i (c f) -> p c i f", f=4),
+            )
+            nc.vector.quantize_mx(
+                out=z_code[:].bitcast(E4M3X4), scales=z_plane[:], in_=z_bf[:].rearrange("p j i -> p (j i)")
+            )
+            for n0 in range(0, N_TILES, 2):
+                bank = psum.tile([P, BANK], F32, name="bank")
+                for s in range(2):
+                    n = n0 + s
+                    nc.tensor.matmul_mx(
+                        out=bank[:, s * CHUNK : (s + 1) * CHUNK],
+                        lhsT=w2_code[:, 2 * n * P : 2 * (n + 1) * P].bitcast(E2M1X4),
+                        lhsT_scale=w2_plane[:, n * P : (n + 1) * P],
+                        rhs=z_code[:].bitcast(E4M3X4),
+                        rhs_scale=z_plane[:],
+                        start=True,
+                        stop=True,
+                    )
+                pair = res[:, n0 : n0 + 2, cols]
+                nc.vector.tensor_tensor(pair, bank[:].rearrange("p (s j) -> p s j", s=2), pair, ALU.mult)
+                nc.sync.dma_start(out=out_tiles[:, n0 : n0 + 2, cols], in_=pair)

@@ -91,12 +91,12 @@ def tile_list_seat_coverage_tuner_kernel(
             nc.sync.dma_start(out=w1_second[u][:], in_=w1_rows[1][:, :, u * (H // 2) : (u + 1) * (H // 2)])
         nc.sync.dma_start(out=wgs_sb[:], in_=wgs)
         nc.sync.dma_start(out=idx2[:], in_=offs2)
+        nc.sync.dma_start(out=idx3[:], in_=offs3)
+        nc.sync.dma_start(out=gain_sb[:], in_=gain.rearrange("(p i) -> p i", i=PACK))
         for a in range(PASSES):
             load_words(w3_code[a], w3_words[a])
         load_scale_rows(w3_plane, w3_scales, PASSES)
-        nc.sync.dma_start(out=idx3[:], in_=offs3)
         nc.sync.dma_start(out=mat_sb[:], in_=mat.rearrange("(p i) j -> p i j", i=PACK))
-        nc.sync.dma_start(out=gain_sb[:], in_=gain.rearrange("(p i) -> p i", i=PACK))
         nc.sync.dma_start(out=w2_code[:].bitcast(I32), in_=w2_words[0].bitcast(I32))
         load_scale_rows(w2_plane, w2_scales, 1)
 
@@ -148,56 +148,71 @@ def tile_list_seat_coverage_tuner_kernel(
         def cosine_of_magnitude(dst, magnitude):
             nc.scalar.activation(out=dst, in_=magnitude, func=ACT.Sin, scale=-1.0, bias=math.pi / 2)
 
-        w3_planes = [w3_plane[4 * a :, :] for a in range(PASSES)]
-        for n in range(N_TILES):
-            for cols in halves:
-                bank = times_table(w3_code, w3_planes, n, cols)
-                nc.scalar.activation(out=mag[n % 2][:, cols], in_=bank[:], func=ACT.Abs)
-            cosine_of_magnitude(res[:, n, :], mag[n % 2][:])
+        def weigh(engine, i, cols):
+            engine.tensor_tensor(h[i][:, cols], h[i][:, cols], wgs_sb[:, cols], ALU.mult)
 
         def put(i, start, count):
-            cols = slice(start, start + count)
-            nc.vector.tensor_tensor(
-                page[i][:].indirect(entries(idx2, start, count)), h[i][:, cols], wgs_sb[:, cols], ALU.mult
-            )
+            nc.vector.tensor_copy(page[i][:].indirect(entries(idx2, start, count)), h[i][:, start : start + count])
 
         def fetch(i, start, count):
             nc.vector.tensor_copy(x[:, i, start : start + count], page[i][:].indirect(entries(idx3, start, count)))
 
+        whole = slice(0, S)
+        weigh(nc.vector, 0, halves[0])
+        for i, cols in ((1, halves[0]), (0, halves[1]), (1, halves[1]), (2, whole), (3, whole)):
+            weigh(nc.gpsimd, i, cols)
         for u in range(2):
             put(0, u * BANK, BANK)
             put(1, u * BANK, BANK)
-        put(2, 0, S)
         fetch(0, 0, S)
         fetch(1, 0, S)
+        put(2, 0, S)
         fetch(2, 0, S)
         put(3, 0, S)
         for u in range(2):
             fetch(3, u * BANK, BANK)
 
-        def combine(i0, i1, cols):
-            nc.vector.tensor_tensor(z[:, i0:i1, cols], z[:, i0:i1, cols], mat_sb[:, i0:i1, cols], ALU.mult)
-            for i in range(i0, i1):
-                nc.vector.scalar_tensor_tensor(
-                    z[:, i, cols], x[:, i, cols], gain_sb[:, i : i + 1], z[:, i, cols], ALU.mult, ALU.add
-                )
+        w3_planes = [w3_plane[4 * a :, :] for a in range(PASSES)]
 
-        whole = slice(0, S)
+        def phase_cosine(n, magnitude):
+            for cols in halves:
+                bank = times_table(w3_code, w3_planes, n, cols)
+                nc.scalar.activation(out=magnitude[:, cols], in_=bank[:], func=ACT.Abs)
+            cosine_of_magnitude(res[:, n, :], magnitude[:])
 
-        def cosine(i, cols):
-            nc.scalar.activation(out=mag[i % 2][:, cols], in_=x[:, i, cols], func=ACT.Abs)
-            cosine_of_magnitude(z[:, i, cols], mag[i % 2][:, cols])
+        def slot_cosine(i, cols, magnitude):
+            nc.scalar.activation(out=magnitude[:, cols], in_=x[:, i, cols], func=ACT.Abs)
+            cosine_of_magnitude(z[:, i, cols], magnitude[:, cols])
 
-        for i in range(3):
-            cosine(i, whole)
+        def combine_early(i):
+            nc.gpsimd.tensor_scalar(x[:, i, :], x[:, i, :], gain_sb[:, i : i + 1], 0.0, ALU.mult, ALU.add)
+            nc.gpsimd.tensor_tensor(z[:, i, :], z[:, i, :], mat_sb[:, i, :], ALU.mult)
+            nc.gpsimd.tensor_tensor(z[:, i, :], z[:, i, :], x[:, i, :], ALU.add)
+
+        def combine_last(cols):
+            i = PACK - 1
+            nc.vector.tensor_tensor(z[:, i, cols], z[:, i, cols], mat_sb[:, i, cols], ALU.mult)
+            nc.vector.scalar_tensor_tensor(
+                z[:, i, cols], x[:, i, cols], gain_sb[:, i : i + 1], z[:, i, cols], ALU.mult, ALU.add
+            )
+
+        for n in range(4):
+            phase_cosine(n, mag[n % 2])
+        slot_cosine(0, whole, mag[0])
+        combine_early(0)
+        phase_cosine(4, mag[1])
+        slot_cosine(1, whole, mag[0])
+        combine_early(1)
+        phase_cosine(5, mag[1])
+        slot_cosine(2, whole, mag[0])
+        combine_early(2)
         chunks = [slice(c, c + CHUNK) for c in range(0, S, CHUNK)]
         for cols in chunks:
-            cosine(3, cols)
-        combine(0, 2, whole)
+            slot_cosine(3, cols, mag[1])
 
         out_tiles = out.rearrange("(n p) j -> p n j", p=P)
         for c, cols in enumerate(chunks):
-            combine(2, 4, cols)
+            combine_last(cols)
             z_bf = held("z_bf%d" % c, [P, CHUNK, PACK], BF16)
             z_code = held("z_code%d" % c, [P, CHUNK], U32)
             z_plane = held("z_plane%d" % c, [P, CHUNK], U8)

import math
from contextlib import ExitStack

import concourse.mybir as mybir

K, T, S, T2, H, N = 1024, 4096, 1024, 2048, 512, 768
FLOPS = 2 * K * H * S + 2 * K * N * S + 2 * H * N * S

F32 = mybir.dt.float32
BF16 = mybir.dt.bfloat16
I32 = mybir.dt.int32
U32 = mybir.dt.uint32
U16 = mybir.dt.uint16
U8 = mybir.dt.uint8
E4M3X4 = mybir.dt.float8_e4m3fn_x4
E2M1X4 = mybir.dt.float4_e2m1fn_x4
ALU = mybir.AluOpType
ACT = mybir.ActivationFunctionType

P = 128
PACK = 4
PASSES = K // (P * PACK)
BANK = 512
N_TILES = N // P
CHUNK = 256
LIST_ROWS = 16


def tile_list_seat_coverage_tuner_kernel(
    tc, tab_words, tab_scales, offs, offs2, offs3, w1, wgs, mat, gain, w2_words, w2_scales, w3_words, w3_scales, out
):
    nc = tc.nc
    with ExitStack() as ctx:
        keep = ctx.enter_context(tc.tile_pool(name="keep", bufs=1))
        psum = ctx.enter_context(tc.psum_pool(name="psum", bufs=8))

        def held(name, shape, dtype):
            return keep.tile(shape, dtype, name=name, align_bytes=64)

        def entries(lst, start, count):
            return lst[:, start // LIST_ROWS : (start + count) // LIST_ROWS]

        def load_scale_rows(plane, scales, passes):
            for q in range(4):
                nc.sync.dma_start(
                    out=plane[32 * q : 32 * q + 4 * passes, :].bitcast(I32),
                    in_=scales[:, 4 * q : 4 * q + 4, :].bitcast(I32),
                )

        def load_words(tile, words):
            nc.sync.dma_start(out=tile[:].bitcast(I32), in_=words.rearrange("p t i -> p (t i)").bitcast(I32))

        idx = held("idx", [P, S // LIST_ROWS], U16)
        idx2 = held("idx2", [P, S // LIST_ROWS], U16)
        idx3 = held("idx3", [P, S // LIST_ROWS], U16)
        tab_code = [held("tab_code%d" % a, [P, T], U32) for a in range(PASSES)]
        tab_plane = held("tab_plane", [P, T], U8)
        v_code = [held("v_code%d" % a, [P, S], U32) for a in range(PASSES)]
        v_plane = held("v_plane", [P, S], U8)
        w1_first = held("w1_first", [P, PACK, H], F32)
        w1_second = [held("w1_second%d" % u, [P, PACK, H // 2], F32) for u in range(2)]
        w1_bf = [held("w1_bf%d" % a, [P, PACK, P, PACK], BF16) for a in range(PASSES)]
        w1_code = [held("w1_code%d" % a, [P, H], U32) for a in range(PASSES)]
        w1_plane = [held("w1_plane%d" % a, [P, H], U8) for a in range(PASSES)]
        w3_code = [held("w3_code%d" % a, [P, N], U32) for a in range(PASSES)]
        w3_plane = held("w3_plane", [P, N], U8)
        w2_code = held("w2_code", [P, 2 * N], U8)
        w2_plane = held("w2_plane", [P, N], U8)
        wgs_sb = held("wgs_sb", [P, S], F32)
        mat_sb = held("mat_sb", [P, PACK, S], F32)
        gain_sb = held("gain_sb", [P, PACK], F32)
        h = [held("h%d" % i, [P, S], F32) for i in range(PACK)]
        page = [held("page%d" % i, [P, T2], F32) for i in range(PACK)]
        x = held("x", [P, PACK, S], F32)
        z = held("z", [P, PACK, S], F32)
        mag = [held("mag%d" % u, [P, S], F32) for u in range(2)]
        res = held("res", [P, N_TILES, S], F32)

        for plane in (tab_plane, w3_plane, w2_plane):
            nc.vector.memset(plane[:].bitcast(I32), 0)
        for i in range(PACK):
            (nc.vector if i < 2 else nc.gpsimd).memset(page[i][:], 0.0)

        w1_rows = w1.rearrange("(a p j) c -> a p j c", a=PASSES, j=PACK)
        nc.sync.dma_start(out=idx[:], in_=offs)
        load_words(tab_code[0], tab_words[0])
        load_scale_rows(tab_plane, tab_scales, PASSES)
        nc.sync.dma_start(out=w1_first[:], in_=w1_rows[0])
        load_words(tab_code[1], tab_words[1])
        for u in range(2):
            nc.sync.dma_start(out=w1_second[u][:], in_=w1_rows[1][:, :, u * (H // 2) : (u + 1) * (H // 2)])
        nc.sync.dma_start(out=wgs_sb[:], in_=wgs)
        nc.sync.dma_start(out=idx2[:], in_=offs2)
        nc.sync.dma_start(out=idx3[:], in_=offs3)
        nc.sync.dma_start(out=gain_sb[:], in_=gain.rearrange("(p i) -> p i", i=PACK))
        for a in range(PASSES):
            load_words(w3_code[a], w3_words[a])
        load_scale_rows(w3_plane, w3_scales, PASSES)
        nc.sync.dma_start(out=mat_sb[:], in_=mat.rearrange("(p i) j -> p i j", i=PACK))
        nc.sync.dma_start(out=w2_code[:].bitcast(I32), in_=w2_words[0].bitcast(I32))
        load_scale_rows(w2_plane, w2_scales, 1)

        nc.vector.tensor_copy(v_code[0][:], tab_code[0][:].indirect(idx[:]))
        nc.vector.tensor_copy(v_plane[:], tab_plane[:].indirect(idx[:]))

        def deal_w1(copy, a, raw, m0, count):
            copy(
                out=w1_bf[a][:, :, m0 : m0 + count, :].rearrange("p i m j -> p m j i"),
                in_=raw[:].rearrange("p j (m i) -> p m j i", i=PACK),
            )

        def quantise_w1(a, i0, i1):
            cols = slice(i0 * P, i1 * P)
            nc.vector.quantize_mx(
                out=w1_code[a][:, cols].bitcast(E4M3X4),
                scales=w1_plane[a][:, cols],
                in_=w1_bf[a][:, i0:i1, :, :].rearrange("p i m j -> p (i m j)"),
            )

        deal_w1(nc.scalar.copy, 0, w1_first, 0, P)
        quantise_w1(0, 0, PACK)
        nc.vector.tensor_copy(v_code[1][:], tab_code[1][:].indirect(idx[:]))
        deal_w1(nc.scalar.copy, 1, w1_second[0], 0, P // 2)
        deal_w1(nc.vector.tensor_copy, 1, w1_second[1], P // 2, P // 2)
        quantise_w1(1, 0, 1)
        quantise_w1(1, 1, PACK)

        def times_table(codes, planes, tile, cols):
            bank = psum.tile([P, BANK], F32, name="bank")
            m_cols = slice(tile * P, (tile + 1) * P)
            for a in range(PASSES):
                nc.tensor.matmul_mx(
                    out=bank[:],
                    lhsT=codes[a][:, m_cols].bitcast(E4M3X4),
                    lhsT_scale=planes[a][:, m_cols],
                    rhs=v_code[a][:, cols].bitcast(E4M3X4),
                    rhs_scale=v_plane[4 * a :, cols],
                    start=(a == 0),
                    stop=(a == PASSES - 1),
                )
            return bank

        halves = [slice(u * BANK, (u + 1) * BANK) for u in range(S // BANK)]
        for i, u in ((0, 0), (1, 0), (0, 1), (1, 1), (2, 0), (2, 1), (3, 0), (3, 1)):
            bank = times_table(w1_code, w1_plane, i, halves[u])
            nc.scalar.activation(out=h[i][:, halves[u]], in_=bank[:], func=ACT.Gelu_apprx_tanh)

        def cosine_of_magnitude(dst, magnitude):
            nc.scalar.activation(out=dst, in_=magnitude, func=ACT.Sin, scale=-1.0, bias=math.pi / 2)

        def weigh(engine, i, cols):
            engine.tensor_tensor(h[i][:, cols], h[i][:, cols], wgs_sb[:, cols], ALU.mult)

        def put(i, start, count):
            nc.vector.tensor_copy(page[i][:].indirect(entries(idx2, start, count)), h[i][:, start : start + count])

        def fetch(i, start, count):
            nc.vector.tensor_copy(x[:, i, start : start + count], page[i][:].indirect(entries(idx3, start, count)))

        whole = slice(0, S)
        weigh(nc.vector, 0, halves[0])
        for i, cols in ((1, halves[0]), (0, halves[1]), (1, halves[1]), (2, whole), (3, whole)):
            weigh(nc.gpsimd, i, cols)
        for u in range(2):
            put(0, u * BANK, BANK)
            put(1, u * BANK, BANK)
        fetch(0, 0, S)
        fetch(1, 0, S)
        put(2, 0, S)
        fetch(2, 0, S)
        put(3, 0, S)
        for u in range(2):
            fetch(3, u * BANK, BANK)

        w3_planes = [w3_plane[4 * a :, :] for a in range(PASSES)]

        def phase_cosine(n, magnitude):
            for cols in halves:
                bank = times_table(w3_code, w3_planes, n, cols)
                nc.scalar.activation(out=magnitude[:, cols], in_=bank[:], func=ACT.Abs)
            cosine_of_magnitude(res[:, n, :], magnitude[:])

        def slot_cosine(i, cols, magnitude):
            nc.scalar.activation(out=magnitude[:, cols], in_=x[:, i, cols], func=ACT.Abs)
            cosine_of_magnitude(z[:, i, cols], magnitude[:, cols])

        def combine_early(i):
            nc.gpsimd.tensor_scalar(x[:, i, :], x[:, i, :], gain_sb[:, i : i + 1], 0.0, ALU.mult, ALU.add)
            nc.gpsimd.tensor_tensor(z[:, i, :], z[:, i, :], mat_sb[:, i, :], ALU.mult)
            nc.gpsimd.tensor_tensor(z[:, i, :], z[:, i, :], x[:, i, :], ALU.add)

        def combine_last(cols):
            i = PACK - 1
            nc.vector.tensor_tensor(z[:, i, cols], z[:, i, cols], mat_sb[:, i, cols], ALU.mult)
            nc.vector.scalar_tensor_tensor(
                z[:, i, cols], x[:, i, cols], gain_sb[:, i : i + 1], z[:, i, cols], ALU.mult, ALU.add
            )

        for n in range(4):
            phase_cosine(n, mag[n % 2])
        slot_cosine(0, whole, mag[0])
        combine_early(0)
        phase_cosine(4, mag[1])
        slot_cosine(1, whole, mag[0])
        combine_early(1)
        phase_cosine(5, mag[1])
        slot_cosine(2, whole, mag[0])
        combine_early(2)
        chunks = [slice(c, c + CHUNK) for c in range(0, S, CHUNK)]
        for cols in chunks:
            slot_cosine(3, cols, mag[1])

        out_tiles = out.rearrange("(n p) j -> p n j", p=P)
        for c, cols in enumerate(chunks):
            combine_last(cols)
            z_bf = held("z_bf%d" % c, [P, CHUNK, PACK], BF16)
            z_code = held("z_code%d" % c, [P, CHUNK], U32)
            z_plane = held("z_plane%d" % c, [P, CHUNK], U8)
            nc.scalar.copy(
                out=z_bf[:].rearrange("p (c f) i -> p c i f", f=4),
                in_=z[:, :, cols].rearrange("p i (c f) -> p c i f", f=4),
            )
            nc.vector.quantize_mx(
                out=z_code[:].bitcast(E4M3X4), scales=z_plane[:], in_=z_bf[:].rearrange("p j i -> p (j i)")
            )
            for n0 in range(0, N_TILES, 2):
                bank = psum.tile([P, BANK], F32, name="bank")
                for s in range(2):
                    n = n0 + s
                    nc.tensor.matmul_mx(
                        out=bank[:, s * CHUNK : (s + 1) * CHUNK],
                        lhsT=w2_code[:, 2 * n * P : 2 * (n + 1) * P].bitcast(E2M1X4),
                        lhsT_scale=w2_plane[:, n * P : (n + 1) * P],
                        rhs=z_code[:].bitcast(E4M3X4),
                        rhs_scale=z_plane[:],
                        start=True,
                        stop=True,
                    )
                pair = res[:, n0 : n0 + 2, cols]
                nc.vector.tensor_tensor(pair, bank[:].rearrange("p (s j) -> p s j", s=2), pair, ALU.mult)
                nc.sync.dma_start(out=out_tiles[:, n0 : n0 + 2, cols], in_=pair)
